import numpy as np
import ml_dtypes


def mxq(x, axis, fmt="e4m3"):
    dtype, down = {"e4m3": (ml_dtypes.float8_e4m3fn, 7), "e5m2": (ml_dtypes.float8_e5m2, 14)}[fmt]
    v = np.moveaxis(np.asarray(x, np.float32).astype(ml_dtypes.bfloat16).astype(np.float64), axis, -1)
    blocks = v.reshape(v.shape[:-1] + (-1, 32))
    amax = np.abs(blocks).max(-1, keepdims=True)
    byte = np.maximum(np.where(amax > 0, np.frexp(amax)[1] - 1 + 127, 0) - down, 1)
    scale = np.exp2(byte - 127.0)
    codes = (blocks / scale).astype(np.float32).astype(dtype).astype(np.float64)
    return np.moveaxis((codes * scale).reshape(v.shape), -1, axis)


WIDE = False


def mx_kscale(k):
    if not WIDE:
        return np.ones(k)
    levels = np.array([30, -30])
    if k % 512:
        return np.exp2(np.random.permutation(np.resize(levels, k // 32))).repeat(32)
    a = np.empty((k // 512, 16))
    for p in range(k // 512):
        a[p, :8] = np.random.permutation(np.resize(levels, 8))
        for g in range(8):
            far = levels[np.abs(levels - a[p, g]) >= 10]
            a[p, g + 8] = far[np.random.randint(len(far))]
    return np.exp2(a.ravel()).repeat(32)


def f64(x):
    return np.asarray(x).astype(np.float64)


def striped(idx):
    return np.tile(np.asarray(idx).reshape(-1, 16).T, (8, 1)).astype(np.uint16)


def unstriped(offs):
    return offs[:16].T.reshape(-1).astype(np.int64)


E2M1 = np.array([0.0, 0.5, 1.0, 1.5, 2.0, 3.0, 4.0, 6.0, -0.0, -0.5, -1.0, -1.5, -2.0, -3.0, -4.0, -6.0])


def pack_weight(w, fmt):
    k, n = w.shape
    w = f64(np.asarray(w, np.float32).astype(ml_dtypes.bfloat16)).reshape(k // 32, 32, n)
    amax = np.abs(w).max(1)
    if fmt in ("e4m3", "e5m2"):
        byte = np.frexp(amax)[1] - 1 + 127 - (7 if fmt == "e4m3" else 14)
    else:
        mant, ex = np.frexp(amax / 6.0)
        byte = np.where(mant > 0.5, ex, ex - 1) + 127
    byte = np.clip(np.where(amax > 0, byte, 1), 1, 254)
    scaled = (w * np.exp2(127.0 - byte)[:, None, :]).reshape(k, n).astype(np.float32)
    by_word = np.ascontiguousarray(scaled.reshape(k // 512, 128, 4, n).transpose(0, 1, 3, 2))
    if fmt in ("e4m3", "e5m2"):
        words = by_word.astype(ml_dtypes.float8_e4m3fn if fmt == "e4m3" else ml_dtypes.float8_e5m2).view(np.uint8)
    else:
        c = by_word.astype(ml_dtypes.float4_e2m1fn).view(np.uint8) & 0xF
        words = (c[..., 0::2] | (c[..., 1::2] << 4)).reshape(k // 512, 128, 2 * n)
    return np.ascontiguousarray(words), np.ascontiguousarray(byte.astype(np.uint8).reshape(k // 512, 16, n))


def unpack_weight(words, scales, fmt):
    g, _, n = scales.shape
    words = np.ascontiguousarray(words).reshape(g, 128, n, -1)
    if fmt in ("e4m3", "e5m2"):
        vals = words.view(ml_dtypes.float8_e4m3fn if fmt == "e4m3" else ml_dtypes.float8_e5m2).astype(np.float64)
    else:
        nib = np.empty((g, 128, n, 4), np.uint8)
        nib[..., 0::2] = words & 0xF
        nib[..., 1::2] = words >> 4
        vals = E2M1[nib]
    vals = vals * np.repeat(np.exp2(scales.astype(np.float64) - 127.0), 8, axis=1)[..., None]
    return vals.transpose(0, 1, 3, 2).reshape(g * 512, n)


def sigmoid(v):
    return 1.0 / (1.0 + np.exp(-v))


def sgn(shape):
    return np.random.uniform(0.5, 2.0, shape) * np.where(np.random.standard_normal(shape) < 0, -1.0, 1.0)


K, T, J, R, F, Z, N, O = 512, 1024, 256, 512, 512, 1024, 256, 128


def setup_inputs():
    n = np.random.standard_normal
    idx = np.random.permutation(T)[:J]
    idx2 = np.random.permutation(Z)[:J]
    idx3 = np.random.permutation(J)[:O]
    idx4 = np.random.permutation(J)[:O]
    idx5 = np.random.permutation(J)[:O]
    idx6 = np.random.permutation(J)[:O]
    fk = mx_kscale(K)
    ff = mx_kscale(F)
    fr = mx_kscale(R)
    xtp = pack_weight(n((K, T)) / fk[:, None], "e4m3")
    xop = pack_weight(n((F, Z)) / ff[:, None], "e2m1")
    wp = pack_weight(n((K, R)) * 1 / np.sqrt(K) * fk[:, None] * fr, "e2m1")
    w2p = pack_weight(n((F, R)) * 1 / np.sqrt(F) * ff[:, None] * fr, "e5m2")
    wbp = pack_weight(n((R, N)) * 1 / np.sqrt(R) / fr[:, None], "e5m2")
    wcp = pack_weight(n((R, N)) * 1 / np.sqrt(R) / fr[:, None], "e2m1")
    return {
        "xt_words": xtp[0],
        "xt_scales": xtp[1],
        "xo_words": xop[0],
        "xo_scales": xop[1],
        "w_words": wp[0],
        "w_scales": wp[1],
        "w2_words": w2p[0],
        "w2_scales": w2p[1],
        "wb_words": wbp[0],
        "wb_scales": wbp[1],
        "wc_words": wcp[0],
        "wc_scales": wcp[1],
        "so": (np.random.uniform(0.5, 1.6, (N, 1))).astype(np.float32),
        "sp": (sgn((N, 1))).astype(np.float32),
        "bo": (np.random.uniform(-2.0, 2.0, (N, 1))).astype(np.float32),
        "so2": (np.random.uniform(0.5, 1.6, (N, 1))).astype(np.float32),
        "sp2": (sgn((N, 1))).astype(np.float32),
        "bo2": (np.random.uniform(-2.0, 2.0, (N, 1))).astype(np.float32),
        "offs": striped(idx),
        "offs2": striped(idx2),
        "offs3": striped(idx3),
        "offs4": striped(idx4),
        "offs5": striped(idx5),
        "offs6": striped(idx6),
    }


def reference(xt_words, xt_scales, xo_words, xo_scales, w_words, w_scales, w2_words, w2_scales, wb_words, wb_scales, wc_words, wc_scales, so, sp, bo, so2, sp2, bo2, offs, offs2, offs3, offs4, offs5, offs6):
    idx = unstriped(offs)
    idx2 = unstriped(offs2)
    idx3 = unstriped(offs3)
    idx4 = unstriped(offs4)
    idx5 = unstriped(offs5)
    idx6 = unstriped(offs6)
    xtu = unpack_weight(xt_words, xt_scales, "e4m3")
    xou = unpack_weight(xo_words, xo_scales, "e2m1")
    wu = unpack_weight(w_words, w_scales, "e2m1")
    w2u = unpack_weight(w2_words, w2_scales, "e5m2")
    wbu = unpack_weight(wb_words, wb_scales, "e5m2")
    wcu = unpack_weight(wc_words, wc_scales, "e2m1")
    xtidxg = xtu[:, idx]
    a = wu.T @ xtidxg
    xoidx2g = xou[:, idx2]
    b = w2u.T @ xoidx2g
    hid = np.maximum(a, b)
    hidq = mxq(hid, 0, "e4m3")
    p = wbu.T @ hidq
    q = wcu.T @ hidq
    y = p[:, idx3] * f64(so) * sigmoid(q[:, idx4] * f64(sp) + f64(bo)) - q[:, idx5] * f64(so2) * sigmoid(p[:, idx6] * f64(sp2) + f64(bo2))
    return y

@@ -1,0 +1,206 @@
+from contextlib import ExitStack
+
+import concourse.mybir as mybir
+
+K, T, J, R, F, Z, N, O = 512, 1024, 256, 512, 512, 1024, 256, 128
+FLOPS = 2 * K * R * J + 2 * F * R * J + 2 * 2 * R * N * J
+
+F32 = mybir.dt.float32
+BF16 = mybir.dt.bfloat16
+I32 = mybir.dt.int32
+U32 = mybir.dt.uint32
+U16 = mybir.dt.uint16
+U8 = mybir.dt.uint8
+E4M3 = mybir.dt.float8_e4m3fn_x4
+E5M2 = mybir.dt.float8_e5m2_x4
+E2M1 = mybir.dt.float4_e2m1fn_x4
+ACT = mybir.ActivationFunctionType
+ALU = mybir.AluOpType
+
+P = 128
+PACK = 4
+HALF = 128
+
+
+def tile_list_outcomegatedcross_twotab_kernel(
+    tc, xt_words, xt_scales, xo_words, xo_scales, w_words, w_scales, w2_words, w2_scales,
+    wb_words, wb_scales, wc_words, wc_scales, so, sp, bo, so2, sp2, bo2,
+    offs, offs2, offs3, offs4, offs5, offs6, out,
+):
+    nc = tc.nc
+    with ExitStack() as ctx:
+        sb = ctx.enter_context(tc.tile_pool(name="sb", bufs=1))
+        ps = ctx.enter_context(tc.psum_pool(name="ps", bufs=1))
+
+        def tile(name, shape, dtype):
+            return sb.tile(shape, dtype, name=name, align_bytes=64)
+
+        def load_list(name, src):
+            t = tile(name, list(src.shape), U16)
+            nc.sync.dma_start(t[:], src)
+            return t
+
+        def load_words8(name, src, cols, queue):
+            t = tile(name, [P, cols], U32)
+            queue.dma_start(t[:].bitcast(I32), src[0].rearrange("p n t -> p (n t)").bitcast(I32))
+            return t
+
+        def load_words4(name, src, cols, queue):
+            t = tile(name, [P, cols], U16)
+            queue.dma_start(t[:].bitcast(I32), src[0].bitcast(I32))
+            return t
+
+        def cleared_plane(name, cols, engine):
+            t = tile(name, [P, cols], U8)
+            engine.memset(t[:].bitcast(I32), 0)
+            return t
+
+        def load_plane(t, src, queue):
+            for q in range(4):
+                queue.dma_start(t[32 * q : 32 * q + 4, :].bitcast(I32), src[0, 4 * q : 4 * q + 4, :].bitcast(I32))
+
+        def load_folded(t, start, src, queue):
+            cols = src.shape[2]
+            both = t[:].bitcast(I32).rearrange("p (a c) -> p a c", a=2)
+            quads = src[0].bitcast(I32).rearrange("(a b r) c -> b r a c", a=2, b=2)
+            for b in range(2):
+                queue.dma_start(both[32 * b : 32 * b + 4, :, start // 4 : (start + cols) // 4], quads[b])
+
+        def unfold(t, width):
+            words = t[:].bitcast(I32)
+            nc.vector.tensor_copy(words[64:128, 0 : width // 4], words[0:64, width // 4 : width // 2])
+
+        xo_f = cleared_plane("xo_f", 2 * Z, nc.vector)
+        s1 = cleared_plane("s1", 4 * R, nc.gpsimd)
+        xt_s = cleared_plane("xt_s", T, nc.vector)
+        s2 = cleared_plane("s2", 4 * N, nc.gpsimd)
+
+        xo_w = load_words4("xo_w", xo_words, Z, nc.scalar)
+        xt_w = load_words8("xt_w", xt_words, T, nc.scalar)
+        l2 = load_list("l2", offs2)
+        l1 = load_list("l1", offs)
+        load_folded(xo_f, 0, xo_scales, nc.sync)
+        load_folded(s1, 0, w2_scales, nc.sync)
+        w2_w = load_words8("w2_w", w2_words, R, nc.sync)
+        load_folded(s1, R, w_scales, nc.sync)
+        w_w = load_words4("w_w", w_words, R, nc.sync)
+        load_plane(xt_s, xt_scales, nc.sync)
+        wb_w = load_words8("wb_w", wb_words, N, nc.sync)
+        wc_w = load_words4("wc_w", wc_words, N, nc.sync)
+        load_folded(s2, 0, wb_scales, nc.sync)
+        load_folded(s2, N, wc_scales, nc.sync)
+        l6 = load_list("l6", offs6)
+        l3 = load_list("l3", offs3)
+        l4 = load_list("l4", offs4)
+        l5 = load_list("l5", offs5)
+        rows = {}
+        for name, src in (("sp2", sp2), ("bo2", bo2), ("so", so), ("sp", sp), ("bo", bo), ("so2", so2)):
+            t = tile(name, [P, 2], F32)
+            with nc.allow_non_contiguous_dma(reason="one value a partition"):
+                nc.sync.dma_start(t[:], src.rearrange("(h p) o -> p (h o)", p=P))
+            rows[name] = t
+
+        def gather(name, window, offsets, dtype):
+            t = tile(name, [P, J], dtype)
+            nc.vector.tensor_copy(t[:], window[:].indirect(offsets[:]))
+            return t
+
+        def dealt(name, src, dtype, copy):
+            t = tile(name, [P, R], dtype)
+            copy(t[:].rearrange("p (t m) -> p m t", t=PACK), src.rearrange("p (m t) -> p m t", t=PACK))
+            return t
+
+        xo_s = tile("xo_s", [P, Z], U8)
+        for a in range(2):
+            nc.vector.tensor_copy(
+                xo_s[64 * a : 64 * a + 64, :].bitcast(I32), xo_f[0:64, a * Z : (a + 1) * Z].bitcast(I32)
+            )
+        xo_gs = gather("xo_gs", xo_s, l2, U8)
+        xo_g = gather("xo_g", xo_w, l2, U16)
+        unfold(s1, 2 * R)
+        w2_d = dealt("w2_d", w2_w[:], U32, nc.scalar.copy)
+        w2_ds = dealt("w2_ds", s1[:, 0:R], U8, nc.vector.tensor_copy)
+        w_d = dealt("w_d", w_w[:], U16, nc.scalar.copy)
+        w_ds = dealt("w_ds", s1[:, R : 2 * R], U8, nc.vector.tensor_copy)
+        xt_g = tile("xt_g", [P, J], U32)
+        xt_gs = tile("xt_gs", [P, J], U8)
+        for h in range(2):
+            part = l1[:, h * HALF // 16 : (h + 1) * HALF // 16]
+            nc.vector.tensor_copy(xt_g[:, h * HALF : (h + 1) * HALF], xt_w[:].indirect(part))
+            nc.vector.tensor_copy(xt_gs[:, h * HALF : (h + 1) * HALF], xt_s[:].indirect(part))
+        unfold(s2, 2 * N)
+        wb_s = s2[:, 0:N]
+        wc_s = s2[:, N : 2 * N]
+
+        def first_stage(name, wd, wds, wfmt, xg, xgs, xfmt, h):
+            acc = ps.tile([P, PACK, HALF], F32, name=name)
+            js = slice(h * HALF, (h + 1) * HALF)
+            for t in range(PACK):
+                ms = slice(t * P, (t + 1) * P)
+                nc.tensor.matmul_mx(
+                    out=acc[:, t, :], lhsT=wd[:, ms].bitcast(wfmt), lhsT_scale=wds[:, ms],
+                    rhs=xg[:, js].bitcast(xfmt), rhs_scale=xgs[:, js], start=True, stop=True,
+                )
+            return acc
+
+        b_sb = []
+        for h in range(2):
+            acc = first_stage("b_ps%d" % h, w2_d, w2_ds, E5M2, xo_g, xo_gs, E2M1, h)
+            t = tile("b_sb%d" % h, [P, HALF, PACK], F32)
+            nc.scalar.copy(t[:], acc[:].rearrange("p t j -> p j t"))
+            b_sb.append(t)
+        hid = []
+        for h in range(2):
+            acc = first_stage("a_ps%d" % h, w_d, w_ds, E2M1, xt_g, xt_gs, E4M3, h)
+            t = tile("hid%d" % h, [P, HALF, PACK], BF16)
+            nc.vector.tensor_tensor(t[:], acc[:].rearrange("p t j -> p j t"), b_sb[h][:], ALU.max)
+            hid.append(t)
+        hq = []
+        for h in range(2):
+            c = tile("hq%d" % h, [P, HALF], U32)
+            s = tile("hs%d" % h, [P, HALF], U8)
+            nc.vector.quantize_mx(out=c[:].bitcast(E4M3), scales=s[:], in_=hid[h][:].rearrange("p j t -> p (j t)"))
+            hq.append((c, s))
+
+        outcome_ps = {}
+        for g in range(2):
+            for name in ("p", "q"):
+                outcome_ps[name, g] = ps.tile([P, J], F32, name="%s_ps%d" % (name, g))
+        for g in range(2):
+            ns = slice(g * P, (g + 1) * P)
+            for name, ww, ws, fmt in (("p", wb_w, wb_s, E5M2), ("q", wc_w, wc_s, E2M1)):
+                for h in range(2):
+                    js = slice(h * HALF, (h + 1) * HALF)
+                    nc.tensor.matmul_mx(
+                        out=outcome_ps[name, g][:, js], lhsT=ww[:, ns].bitcast(fmt), lhsT_scale=ws[:, ns],
+                        rhs=hq[h][0][:].bitcast(E4M3), rhs_scale=hq[h][1][:], start=True, stop=True,
+                    )
+
+        outcome = {}
+        for g in range(2):
+            for name in ("p", "q"):
+                t = tile("%s_sb%d" % (name, g), [P, J], F32)
+                nc.vector.tensor_copy(t[:], outcome_ps[name, g][:])
+                outcome[name, g] = t
+
+        for g in range(2):
+            col = slice(g, g + 1)
+            gate2 = tile("gate2_%d" % g, [P, O], F32)
+            nc.scalar.activation(out=gate2[:], in_=outcome["p", g][:].indirect(l6[:]), func=ACT.Sigmoid,
+                                 bias=rows["bo2"][:, col], scale=rows["sp2"][:, col])
+            val1 = tile("val1_%d" % g, [P, O], F32)
+            nc.scalar.activation(out=val1[:], in_=outcome["p", g][:].indirect(l3[:]), func=ACT.Copy,
+                                 scale=rows["so"][:, col])
+            gate1 = tile("gate1_%d" % g, [P, O], F32)
+            nc.scalar.activation(out=gate1[:], in_=outcome["q", g][:].indirect(l4[:]), func=ACT.Sigmoid,
+                                 bias=rows["bo"][:, col], scale=rows["sp"][:, col])
+            val2 = tile("val2_%d" % g, [P, O], F32)
+            nc.scalar.activation(out=val2[:], in_=outcome["q", g][:].indirect(l5[:]), func=ACT.Copy,
+                                 scale=rows["so2"][:, col])
+            t1 = tile("t1_%d" % g, [P, O], F32)
+            nc.vector.tensor_tensor(t1[:], val1[:], gate1[:], ALU.mult)
+            t2 = tile("t2_%d" % g, [P, O], F32)
+            nc.vector.tensor_tensor(t2[:], val2[:], gate2[:], ALU.mult)
+            y = tile("y_%d" % g, [P, O], F32)
+            nc.vector.tensor_tensor(y[:], t1[:], t2[:], ALU.subtract)
+            nc.sync.dma_start(out[g * P : (g + 1) * P, :], y[:])

@@ -70,18 +70,24 @@ def tile_list_outcomegatedcross_twotab_kernel(
             words = t[:].bitcast(I32)
             nc.vector.tensor_copy(words[64:128, 0 : width // 4], words[0:64, width // 4 : width // 2])
 
-        xo_f = cleared_plane("xo_f", 2 * Z, nc.vector)
-        s1 = cleared_plane("s1", 4 * R, nc.gpsimd)
-        xt_s = cleared_plane("xt_s", T, nc.vector)
-        s2 = cleared_plane("s2", 4 * N, nc.gpsimd)
+        def load_rows(name, src):
+            t = tile(name, [P, 2], F32)
+            with nc.allow_non_contiguous_dma(reason="one value a partition"):
+                nc.sync.dma_start(t[:], src.rearrange("(h p) o -> p (h o)", p=P))
+            return t
 
-        xo_w = load_words4("xo_w", xo_words, Z, nc.scalar)
-        xt_w = load_words8("xt_w", xt_words, T, nc.scalar)
+        xo_s = cleared_plane("xo_s", Z, nc.vector)
+        s1 = cleared_plane("s1", 4 * R, nc.vector)
+        xt_s = cleared_plane("xt_s", T, nc.gpsimd)
+        s2 = cleared_plane("s2", 4 * N, nc.vector)
+
         l2 = load_list("l2", offs2)
         l1 = load_list("l1", offs)
-        load_folded(xo_f, 0, xo_scales, nc.sync)
-        load_folded(s1, 0, w2_scales, nc.sync)
+        load_plane(xo_s, xo_scales, nc.sync)
+        xo_w = load_words4("xo_w", xo_words, Z, nc.sync)
+        xt_w = load_words8("xt_w", xt_words, T, nc.sync)
         w2_w = load_words8("w2_w", w2_words, R, nc.sync)
+        load_folded(s1, 0, w2_scales, nc.sync)
         load_folded(s1, R, w_scales, nc.sync)
         w_w = load_words4("w_w", w_words, R, nc.sync)
         load_plane(xt_s, xt_scales, nc.sync)
@@ -89,44 +95,42 @@ def tile_list_outcomegatedcross_twotab_kernel(
         wc_w = load_words4("wc_w", wc_words, N, nc.sync)
         load_folded(s2, 0, wb_scales, nc.sync)
         load_folded(s2, N, wc_scales, nc.sync)
-        l6 = load_list("l6", offs6)
-        l3 = load_list("l3", offs3)
-        l4 = load_list("l4", offs4)
-        l5 = load_list("l5", offs5)
         rows = {}
-        for name, src in (("sp2", sp2), ("bo2", bo2), ("so", so), ("sp", sp), ("bo", bo), ("so2", so2)):
-            t = tile(name, [P, 2], F32)
-            with nc.allow_non_contiguous_dma(reason="one value a partition"):
-                nc.sync.dma_start(t[:], src.rearrange("(h p) o -> p (h o)", p=P))
-            rows[name] = t
+        l6 = load_list("l6", offs6)
+        rows["sp2"] = load_rows("sp2", sp2)
+        rows["bo2"] = load_rows("bo2", bo2)
+        l3 = load_list("l3", offs3)
+        rows["so"] = load_rows("so", so)
+        l4 = load_list("l4", offs4)
+        rows["sp"] = load_rows("sp", sp)
+        rows["bo"] = load_rows("bo", bo)
+        l5 = load_list("l5", offs5)
+        rows["so2"] = load_rows("so2", so2)
 
         def gather(name, window, offsets, dtype):
             t = tile(name, [P, J], dtype)
             nc.vector.tensor_copy(t[:], window[:].indirect(offsets[:]))
             return t
 
-        def dealt(name, src, dtype, copy):
+        def dealt(name, src, dtype, copy, run):
             t = tile(name, [P, R], dtype)
-            copy(t[:].rearrange("p (t m) -> p m t", t=PACK), src.rearrange("p (m t) -> p m t", t=PACK))
+            copy(
+                t[:].rearrange("p (t c i) -> p c t i", t=PACK, i=run),
+                src.rearrange("p (c i t) -> p c t i", t=PACK, i=run),
+            )
             return t
 
-        xo_s = tile("xo_s", [P, Z], U8)
-        for a in range(2):
-            nc.vector.tensor_copy(
-                xo_s[64 * a : 64 * a + 64, :].bitcast(I32), xo_f[0:64, a * Z : (a + 1) * Z].bitcast(I32)
-            )
         xo_gs = gather("xo_gs", xo_s, l2, U8)
         xo_g = gather("xo_g", xo_w, l2, U16)
+        xt_g = gather("xt_g", xt_w, l1, U32)
         unfold(s1, 2 * R)
-        w2_d = dealt("w2_d", w2_w[:], U32, nc.scalar.copy)
-        w2_ds = dealt("w2_ds", s1[:, 0:R], U8, nc.vector.tensor_copy)
-        w_d = dealt("w_d", w_w[:], U16, nc.scalar.copy)
-        w_ds = dealt("w_ds", s1[:, R : 2 * R], U8, nc.vector.tensor_copy)
-        xt_g = tile("xt_g", [P, J], U32)
+        w2_d = dealt("w2_d", w2_w[:], U32, nc.scalar.copy, 4)
+        w2_ds = dealt("w2_ds", s1[:, 0:R], U8, nc.vector.tensor_copy, P // 2)
+        w_d = dealt("w_d", w_w[:], U16, nc.scalar.copy, 8)
+        w_ds = dealt("w_ds", s1[:, R : 2 * R], U8, nc.vector.tensor_copy, P // 2)
         xt_gs = tile("xt_gs", [P, J], U8)
         for h in range(2):
             part = l1[:, h * HALF // 16 : (h + 1) * HALF // 16]
-            nc.vector.tensor_copy(xt_g[:, h * HALF : (h + 1) * HALF], xt_w[:].indirect(part))
             nc.vector.tensor_copy(xt_gs[:, h * HALF : (h + 1) * HALF], xt_s[:].indirect(part))
         unfold(s2, 2 * N)
         wb_s = s2[:, 0:N]

@@ -55,9 +55,9 @@ def tile_list_outcomegatedcross_twotab_kernel(
             engine.memset(t[:].bitcast(I32), 0)
             return t
 
-        def load_plane(t, src, queue):
+        def load_plane(t, src, queues):
             for q in range(4):
-                queue.dma_start(t[32 * q : 32 * q + 4, :].bitcast(I32), src[0, 4 * q : 4 * q + 4, :].bitcast(I32))
+                queues[q].dma_start(t[32 * q : 32 * q + 4, :].bitcast(I32), src[0, 4 * q : 4 * q + 4, :].bitcast(I32))
 
         def load_folded(t, start, src, queue):
             cols = src.shape[2]
@@ -76,25 +76,27 @@ def tile_list_outcomegatedcross_twotab_kernel(
                 nc.sync.dma_start(t[:], src.rearrange("(h p) o -> p (h o)", p=P))
             return t
 
-        xo_s = cleared_plane("xo_s", Z, nc.vector)
-        s1 = cleared_plane("s1", 4 * R, nc.vector)
+        w2_s = cleared_plane("w2_s", 2 * R, nc.vector)
+        xo_f = cleared_plane("xo_f", 2 * Z, nc.vector)
         xt_s = cleared_plane("xt_s", T, nc.gpsimd)
-        s2 = cleared_plane("s2", 4 * N, nc.vector)
+        w_s = cleared_plane("w_s", 2 * R, nc.vector)
+        wb_s = cleared_plane("wb_s", N, nc.vector)
+        wc_s = cleared_plane("wc_s", N, nc.vector)
 
         l2 = load_list("l2", offs2)
-        l1 = load_list("l1", offs)
-        load_plane(xo_s, xo_scales, nc.sync)
         xo_w = load_words4("xo_w", xo_words, Z, nc.sync)
-        xt_w = load_words8("xt_w", xt_words, T, nc.sync)
+        l1 = load_list("l1", offs)
+        load_folded(w2_s, 0, w2_scales, nc.sync)
         w2_w = load_words8("w2_w", w2_words, R, nc.sync)
-        load_folded(s1, 0, w2_scales, nc.sync)
-        load_folded(s1, R, w_scales, nc.sync)
+        load_folded(xo_f, 0, xo_scales, nc.sync)
         w_w = load_words4("w_w", w_words, R, nc.sync)
-        load_plane(xt_s, xt_scales, nc.sync)
+        xt_w = load_words8("xt_w", xt_words, T, nc.sync)
+        load_folded(w_s, 0, w_scales, nc.sync)
+        load_plane(xt_s, xt_scales, [nc.sync] * 4)
         wb_w = load_words8("wb_w", wb_words, N, nc.sync)
         wc_w = load_words4("wc_w", wc_words, N, nc.sync)
-        load_folded(s2, 0, wb_scales, nc.sync)
-        load_folded(s2, N, wc_scales, nc.sync)
+        load_plane(wb_s, wb_scales, [nc.sync] * 4)
+        load_plane(wc_s, wc_scales, [nc.sync] * 4)
         rows = {}
         l6 = load_list("l6", offs6)
         rows["sp2"] = load_rows("sp2", sp2)
@@ -120,21 +122,24 @@ def tile_list_outcomegatedcross_twotab_kernel(
             )
             return t
 
-        xo_gs = gather("xo_gs", xo_s, l2, U8)
         xo_g = gather("xo_g", xo_w, l2, U16)
-        xt_g = gather("xt_g", xt_w, l1, U32)
-        unfold(s1, 2 * R)
+        unfold(w2_s, R)
+        w2_ds = dealt("w2_ds", w2_s[:, 0:R], U8, nc.vector.tensor_copy, P // 2)
         w2_d = dealt("w2_d", w2_w[:], U32, nc.scalar.copy, 4)
-        w2_ds = dealt("w2_ds", s1[:, 0:R], U8, nc.vector.tensor_copy, P // 2)
+        xo_s = tile("xo_s", [P, Z], U8)
+        for a in range(2):
+            nc.vector.tensor_copy(
+                xo_s[64 * a : 64 * a + 64, :].bitcast(I32), xo_f[0:64, a * Z : (a + 1) * Z].bitcast(I32)
+            )
+        xo_gs = gather("xo_gs", xo_s, l2, U8)
+        unfold(w_s, R)
         w_d = dealt("w_d", w_w[:], U16, nc.scalar.copy, 8)
-        w_ds = dealt("w_ds", s1[:, R : 2 * R], U8, nc.vector.tensor_copy, P // 2)
+        w_ds = dealt("w_ds", w_s[:, 0:R], U8, nc.vector.tensor_copy, P // 2)
+        xt_g = gather("xt_g", xt_w, l1, U32)
         xt_gs = tile("xt_gs", [P, J], U8)
         for h in range(2):
             part = l1[:, h * HALF // 16 : (h + 1) * HALF // 16]
             nc.vector.tensor_copy(xt_gs[:, h * HALF : (h + 1) * HALF], xt_s[:].indirect(part))
-        unfold(s2, 2 * N)
-        wb_s = s2[:, 0:N]
-        wc_s = s2[:, N : 2 * N]
 
         def first_stage(name, wd, wds, wfmt, xg, xgs, xfmt, h):
             acc = ps.tile([P, PACK, HALF], F32, name=name)

@@ -19,7 +19,11 @@ ALU = mybir.AluOpType
 
 P = 128
 PACK = 4
-HALF = 128
+QUADRANT = 32
+SLOTS = J // 2
+LIST_ROWS = 16
+LINE = 16
+BYTE_RUN = P // 2
 
 
 def tile_list_outcomegatedcross_twotab_kernel(
@@ -36,180 +40,187 @@ def tile_list_outcomegatedcross_twotab_kernel(
             return sb.tile(shape, dtype, name=name, align_bytes=64)
 
         def load_list(name, src):
-            t = tile(name, list(src.shape), U16)
-            nc.sync.dma_start(t[:], src)
-            return t
+            offsets = tile(name, list(src.shape), U16)
+            nc.sync.dma_start(offsets[:], src)
+            return offsets
 
-        def load_words8(name, src, cols, queue):
-            t = tile(name, [P, cols], U32)
-            queue.dma_start(t[:].bitcast(I32), src[0].rearrange("p n t -> p (n t)").bitcast(I32))
-            return t
+        def load_fp8_words(name, src, cols):
+            words = tile(name, [P, cols], U32)
+            nc.sync.dma_start(words[:].bitcast(I32), src[0].rearrange("p n t -> p (n t)").bitcast(I32))
+            return words
 
-        def load_words4(name, src, cols, queue):
-            t = tile(name, [P, cols], U16)
-            queue.dma_start(t[:].bitcast(I32), src[0].bitcast(I32))
-            return t
+        def load_fp4_words(name, src, cols):
+            words = tile(name, [P, cols], U16)
+            nc.sync.dma_start(words[:].bitcast(I32), src[0].bitcast(I32))
+            return words
 
-        def cleared_plane(name, cols, engine):
-            t = tile(name, [P, cols], U8)
-            engine.memset(t[:].bitcast(I32), 0)
-            return t
+        def cleared(name, cols, engine):
+            plane = tile(name, [P, cols], U8)
+            engine.memset(plane[:].bitcast(I32), 0)
+            return plane
 
-        def load_plane(t, src, queues):
-            for q in range(4):
-                queues[q].dma_start(t[32 * q : 32 * q + 4, :].bitcast(I32), src[0, 4 * q : 4 * q + 4, :].bitcast(I32))
+        def load_plane(plane, src):
+            for quad in range(4):
+                nc.sync.dma_start(
+                    plane[QUADRANT * quad : QUADRANT * quad + 4, :].bitcast(I32),
+                    src[0, 4 * quad : 4 * quad + 4, :].bitcast(I32),
+                )
 
-        def load_folded(t, start, src, queue):
-            cols = src.shape[2]
-            both = t[:].bitcast(I32).rearrange("p (a c) -> p a c", a=2)
-            quads = src[0].bitcast(I32).rearrange("(a b r) c -> b r a c", a=2, b=2)
-            for b in range(2):
-                queue.dma_start(both[32 * b : 32 * b + 4, :, start // 4 : (start + cols) // 4], quads[b])
+        def load_folded(folded, src):
+            halves = folded[:].bitcast(I32).rearrange("p (side c) -> p side c", side=2)
+            rows = src[0].bitcast(I32).rearrange("(side low i) c -> low i side c", side=2, low=2)
+            for low in range(2):
+                nc.sync.dma_start(halves[QUADRANT * low : QUADRANT * low + 4, :, :], rows[low])
 
-        def unfold(t, width):
-            words = t[:].bitcast(I32)
-            nc.vector.tensor_copy(words[64:128, 0 : width // 4], words[0:64, width // 4 : width // 2])
+        def unfold(folded, cols):
+            words = folded[:].bitcast(I32)
+            nc.vector.tensor_copy(words[P // 2 : P, 0 : cols // 4], words[0 : P // 2, cols // 4 : cols // 2])
 
-        def load_rows(name, src):
-            t = tile(name, [P, 2], F32)
+        def load_factor(name, src):
+            factor = tile(name, [P, N // P], F32)
             with nc.allow_non_contiguous_dma(reason="one value a partition"):
-                nc.sync.dma_start(t[:], src.rearrange("(h p) o -> p (h o)", p=P))
-            return t
+                nc.sync.dma_start(factor[:], src.rearrange("(g p) o -> p (g o)", p=P))
+            return factor
 
-        w2_s = cleared_plane("w2_s", 2 * R, nc.vector)
-        xo_f = cleared_plane("xo_f", 2 * Z, nc.vector)
-        xt_s = cleared_plane("xt_s", T, nc.gpsimd)
-        w_s = cleared_plane("w_s", 2 * R, nc.vector)
-        wb_s = cleared_plane("wb_s", N, nc.vector)
-        wc_s = cleared_plane("wc_s", N, nc.vector)
+        w2_s = cleared("w2_s", 2 * R, nc.vector)
+        xo_folded = tile("xo_f", [P, 2 * Z], U8)
+        nc.gpsimd.memset(xo_folded[:, Z : 2 * Z].bitcast(I32), 0)
+        nc.vector.memset(xo_folded[:, 0:Z].bitcast(I32), 0)
+        w_s = cleared("w_s", 2 * R, nc.vector)
+        xt_s = cleared("xt_s", T, nc.gpsimd)
+        wb_s = cleared("wb_s", N, nc.vector)
+        wc_s = cleared("wc_s", N, nc.vector)
 
-        l2 = load_list("l2", offs2)
-        xo_w = load_words4("xo_w", xo_words, Z, nc.sync)
-        l1 = load_list("l1", offs)
-        load_folded(w2_s, 0, w2_scales, nc.sync)
-        w2_w = load_words8("w2_w", w2_words, R, nc.sync)
-        load_folded(xo_f, 0, xo_scales, nc.sync)
-        w_w = load_words4("w_w", w_words, R, nc.sync)
-        xt_w = load_words8("xt_w", xt_words, T, nc.sync)
-        load_folded(w_s, 0, w_scales, nc.sync)
-        load_plane(xt_s, xt_scales, [nc.sync] * 4)
-        wb_w = load_words8("wb_w", wb_words, N, nc.sync)
-        wc_w = load_words4("wc_w", wc_words, N, nc.sync)
-        load_plane(wb_s, wb_scales, [nc.sync] * 4)
-        load_plane(wc_s, wc_scales, [nc.sync] * 4)
-        rows = {}
-        l6 = load_list("l6", offs6)
-        rows["sp2"] = load_rows("sp2", sp2)
-        rows["bo2"] = load_rows("bo2", bo2)
-        l3 = load_list("l3", offs3)
-        rows["so"] = load_rows("so", so)
-        l4 = load_list("l4", offs4)
-        rows["sp"] = load_rows("sp", sp)
-        rows["bo"] = load_rows("bo", bo)
-        l5 = load_list("l5", offs5)
-        rows["so2"] = load_rows("so2", so2)
+        list2 = load_list("l2", offs2)
+        list1 = load_list("l1", offs)
+        load_folded(w2_s, w2_scales)
+        xo_w = load_fp4_words("xo_w", xo_words, Z)
+        load_folded(xo_folded, xo_scales)
+        w2_w = load_fp8_words("w2_w", w2_words, R)
+        w_w = load_fp4_words("w_w", w_words, R)
+        load_folded(w_s, w_scales)
+        xt_w = load_fp8_words("xt_w", xt_words, T)
+        load_plane(xt_s, xt_scales)
+        wb_w = load_fp8_words("wb_w", wb_words, N)
+        wc_w = load_fp4_words("wc_w", wc_words, N)
+        load_plane(wb_s, wb_scales)
+        load_plane(wc_s, wc_scales)
+        list6 = load_list("l6", offs6)
+        slope2 = load_factor("sp2", sp2)
+        offset2 = load_factor("bo2", bo2)
+        list3 = load_list("l3", offs3)
+        weight1 = load_factor("so", so)
+        list4 = load_list("l4", offs4)
+        slope1 = load_factor("sp", sp)
+        offset1 = load_factor("bo", bo)
+        list5 = load_list("l5", offs5)
+        weight2 = load_factor("so2", so2)
 
         def gather(name, window, offsets, dtype):
-            t = tile(name, [P, J], dtype)
-            nc.vector.tensor_copy(t[:], window[:].indirect(offsets[:]))
-            return t
+            picked = tile(name, [P, J], dtype)
+            nc.vector.tensor_copy(picked[:], window[:].indirect(offsets[:]))
+            return picked
 
-        def dealt(name, src, dtype, copy, run):
-            t = tile(name, [P, R], dtype)
+        def deal(name, src, dtype, copy, run):
+            dealt = tile(name, [P, R], dtype)
             copy(
-                t[:].rearrange("p (t c i) -> p c t i", t=PACK, i=run),
+                dealt[:].rearrange("p (t c i) -> p c t i", t=PACK, i=run),
                 src.rearrange("p (c i t) -> p c t i", t=PACK, i=run),
             )
-            return t
+            return dealt
 
-        xo_g = gather("xo_g", xo_w, l2, U16)
         unfold(w2_s, R)
-        w2_ds = dealt("w2_ds", w2_s[:, 0:R], U8, nc.vector.tensor_copy, P // 2)
-        w2_d = dealt("w2_d", w2_w[:], U32, nc.scalar.copy, 4)
+        w2_dealt_s = deal("w2_ds", w2_s[:, 0:R], U8, nc.vector.tensor_copy, BYTE_RUN)
+        w2_dealt_w = deal("w2_d", w2_w[:], U32, nc.scalar.copy, LINE // 4)
+        xo_picked_w = gather("xo_g", xo_w, list2, U16)
         xo_s = tile("xo_s", [P, Z], U8)
-        for a in range(2):
+        for side in range(2):
             nc.vector.tensor_copy(
-                xo_s[64 * a : 64 * a + 64, :].bitcast(I32), xo_f[0:64, a * Z : (a + 1) * Z].bitcast(I32)
+                xo_s[side * P // 2 : (side + 1) * P // 2, :].bitcast(I32),
+                xo_folded[0 : P // 2, side * Z : (side + 1) * Z].bitcast(I32),
             )
-        xo_gs = gather("xo_gs", xo_s, l2, U8)
+        xo_picked_s = gather("xo_gs", xo_s, list2, U8)
         unfold(w_s, R)
-        w_d = dealt("w_d", w_w[:], U16, nc.scalar.copy, 8)
-        w_ds = dealt("w_ds", w_s[:, 0:R], U8, nc.vector.tensor_copy, P // 2)
-        xt_g = gather("xt_g", xt_w, l1, U32)
-        xt_gs = tile("xt_gs", [P, J], U8)
+        w_dealt_w = deal("w_d", w_w[:], U16, nc.scalar.copy, LINE // 2)
+        w_dealt_s = deal("w_ds", w_s[:, 0:R], U8, nc.vector.tensor_copy, BYTE_RUN)
+        xt_picked_w = gather("xt_g", xt_w, list1, U32)
+        xt_picked_s = tile("xt_gs", [P, J], U8)
         for h in range(2):
-            part = l1[:, h * HALF // 16 : (h + 1) * HALF // 16]
-            nc.vector.tensor_copy(xt_gs[:, h * HALF : (h + 1) * HALF], xt_s[:].indirect(part))
+            part = list1[:, h * SLOTS // LIST_ROWS : (h + 1) * SLOTS // LIST_ROWS]
+            nc.vector.tensor_copy(xt_picked_s[:, h * SLOTS : (h + 1) * SLOTS], xt_s[:].indirect(part))
 
-        def first_stage(name, wd, wds, wfmt, xg, xgs, xfmt, h):
-            acc = ps.tile([P, PACK, HALF], F32, name=name)
-            js = slice(h * HALF, (h + 1) * HALF)
+        def first_stage(name, dealt_w, dealt_s, dealt_fmt, picked_w, picked_s, picked_fmt, h):
+            acc = ps.tile([P, PACK, SLOTS], F32, name=name)
+            js = slice(h * SLOTS, (h + 1) * SLOTS)
             for t in range(PACK):
                 ms = slice(t * P, (t + 1) * P)
                 nc.tensor.matmul_mx(
-                    out=acc[:, t, :], lhsT=wd[:, ms].bitcast(wfmt), lhsT_scale=wds[:, ms],
-                    rhs=xg[:, js].bitcast(xfmt), rhs_scale=xgs[:, js], start=True, stop=True,
+                    out=acc[:, t, :], lhsT=dealt_w[:, ms].bitcast(dealt_fmt), lhsT_scale=dealt_s[:, ms],
+                    rhs=picked_w[:, js].bitcast(picked_fmt), rhs_scale=picked_s[:, js], start=True, stop=True,
                 )
             return acc
 
         b_sb = []
         for h in range(2):
-            acc = first_stage("b_ps%d" % h, w2_d, w2_ds, E5M2, xo_g, xo_gs, E2M1, h)
-            t = tile("b_sb%d" % h, [P, HALF, PACK], F32)
-            nc.scalar.copy(t[:], acc[:].rearrange("p t j -> p j t"))
-            b_sb.append(t)
+            acc = first_stage("b_ps%d" % h, w2_dealt_w, w2_dealt_s, E5M2, xo_picked_w, xo_picked_s, E2M1, h)
+            b_half = tile("b_sb%d" % h, [P, SLOTS, PACK], F32)
+            nc.scalar.copy(b_half[:], acc[:].rearrange("p t j -> p j t"))
+            b_sb.append(b_half)
         hid = []
         for h in range(2):
-            acc = first_stage("a_ps%d" % h, w_d, w_ds, E2M1, xt_g, xt_gs, E4M3, h)
-            t = tile("hid%d" % h, [P, HALF, PACK], BF16)
-            nc.vector.tensor_tensor(t[:], acc[:].rearrange("p t j -> p j t"), b_sb[h][:], ALU.max)
-            hid.append(t)
-        hq = []
+            acc = first_stage("a_ps%d" % h, w_dealt_w, w_dealt_s, E2M1, xt_picked_w, xt_picked_s, E4M3, h)
+            hid_half = tile("hid%d" % h, [P, SLOTS, PACK], BF16)
+            nc.vector.tensor_tensor(hid_half[:], acc[:].rearrange("p t j -> p j t"), b_sb[h][:], ALU.max)
+            hid.append(hid_half)
+        hid_mx = []
         for h in range(2):
-            c = tile("hq%d" % h, [P, HALF], U32)
-            s = tile("hs%d" % h, [P, HALF], U8)
-            nc.vector.quantize_mx(out=c[:].bitcast(E4M3), scales=s[:], in_=hid[h][:].rearrange("p j t -> p (j t)"))
-            hq.append((c, s))
+            codes = tile("hq%d" % h, [P, SLOTS], U32)
+            scales = tile("hs%d" % h, [P, SLOTS], U8)
+            nc.vector.quantize_mx(
+                out=codes[:].bitcast(E4M3), scales=scales[:], in_=hid[h][:].rearrange("p j t -> p (j t)")
+            )
+            hid_mx.append((codes, scales))
 
         outcome_ps = {}
-        for g in range(2):
+        for g in range(N // P):
             for name in ("p", "q"):
                 outcome_ps[name, g] = ps.tile([P, J], F32, name="%s_ps%d" % (name, g))
-        for g in range(2):
+        for g in range(N // P):
             ns = slice(g * P, (g + 1) * P)
-            for name, ww, ws, fmt in (("p", wb_w, wb_s, E5M2), ("q", wc_w, wc_s, E2M1)):
+            for name, words, plane, fmt in (("p", wb_w, wb_s, E5M2), ("q", wc_w, wc_s, E2M1)):
                 for h in range(2):
-                    js = slice(h * HALF, (h + 1) * HALF)
+                    codes, scales = hid_mx[h]
                     nc.tensor.matmul_mx(
-                        out=outcome_ps[name, g][:, js], lhsT=ww[:, ns].bitcast(fmt), lhsT_scale=ws[:, ns],
-                        rhs=hq[h][0][:].bitcast(E4M3), rhs_scale=hq[h][1][:], start=True, stop=True,
+                        out=outcome_ps[name, g][:, h * SLOTS : (h + 1) * SLOTS],
+                        lhsT=words[:, ns].bitcast(fmt), lhsT_scale=plane[:, ns],
+                        rhs=codes[:].bitcast(E4M3), rhs_scale=scales[:], start=True, stop=True,
                     )
 
         outcome = {}
-        for g in range(2):
+        for g in range(N // P):
             for name in ("p", "q"):
-                t = tile("%s_sb%d" % (name, g), [P, J], F32)
-                nc.vector.tensor_copy(t[:], outcome_ps[name, g][:])
-                outcome[name, g] = t
+                window = tile("%s_sb%d" % (name, g), [P, J], F32)
+                nc.vector.tensor_copy(window[:], outcome_ps[name, g][:])
+                outcome[name, g] = window
 
-        for g in range(2):
+        for g in range(N // P):
             col = slice(g, g + 1)
             gate2 = tile("gate2_%d" % g, [P, O], F32)
-            nc.scalar.activation(out=gate2[:], in_=outcome["p", g][:].indirect(l6[:]), func=ACT.Sigmoid,
-                                 bias=rows["bo2"][:, col], scale=rows["sp2"][:, col])
-            val1 = tile("val1_%d" % g, [P, O], F32)
-            nc.scalar.activation(out=val1[:], in_=outcome["p", g][:].indirect(l3[:]), func=ACT.Copy,
-                                 scale=rows["so"][:, col])
+            nc.scalar.activation(out=gate2[:], in_=outcome["p", g][:].indirect(list6[:]), func=ACT.Sigmoid,
+                                 bias=offset2[:, col], scale=slope2[:, col])
+            value1 = tile("val1_%d" % g, [P, O], F32)
+            nc.scalar.activation(out=value1[:], in_=outcome["p", g][:].indirect(list3[:]), func=ACT.Copy,
+                                 scale=weight1[:, col])
             gate1 = tile("gate1_%d" % g, [P, O], F32)
-            nc.scalar.activation(out=gate1[:], in_=outcome["q", g][:].indirect(l4[:]), func=ACT.Sigmoid,
-                                 bias=rows["bo"][:, col], scale=rows["sp"][:, col])
-            val2 = tile("val2_%d" % g, [P, O], F32)
-            nc.scalar.activation(out=val2[:], in_=outcome["q", g][:].indirect(l5[:]), func=ACT.Copy,
-                                 scale=rows["so2"][:, col])
-            t1 = tile("t1_%d" % g, [P, O], F32)
-            nc.vector.tensor_tensor(t1[:], val1[:], gate1[:], ALU.mult)
-            t2 = tile("t2_%d" % g, [P, O], F32)
-            nc.vector.tensor_tensor(t2[:], val2[:], gate2[:], ALU.mult)
+            nc.scalar.activation(out=gate1[:], in_=outcome["q", g][:].indirect(list4[:]), func=ACT.Sigmoid,
+                                 bias=offset1[:, col], scale=slope1[:, col])
+            value2 = tile("val2_%d" % g, [P, O], F32)
+            nc.scalar.activation(out=value2[:], in_=outcome["q", g][:].indirect(list5[:]), func=ACT.Copy,
+                                 scale=weight2[:, col])
+            gated1 = tile("t1_%d" % g, [P, O], F32)
+            nc.vector.tensor_tensor(gated1[:], value1[:], gate1[:], ALU.mult)
+            gated2 = tile("t2_%d" % g, [P, O], F32)
+            nc.vector.tensor_tensor(gated2[:], value2[:], gate2[:], ALU.mult)
             y = tile("y_%d" % g, [P, O], F32)
-            nc.vector.tensor_tensor(y[:], t1[:], t2[:], ALU.subtract)
+            nc.vector.tensor_tensor(y[:], gated1[:], gated2[:], ALU.subtract)
             nc.sync.dma_start(out[g * P : (g + 1) * P, :], y[:])

from contextlib import ExitStack

import concourse.mybir as mybir

K, T, J, R, F, Z, N, O = 512, 1024, 256, 512, 512, 1024, 256, 128
FLOPS = 2 * K * R * J + 2 * F * R * J + 2 * 2 * R * N * J

F32 = mybir.dt.float32
BF16 = mybir.dt.bfloat16
I32 = mybir.dt.int32
U32 = mybir.dt.uint32
U16 = mybir.dt.uint16
U8 = mybir.dt.uint8
E4M3 = mybir.dt.float8_e4m3fn_x4
E5M2 = mybir.dt.float8_e5m2_x4
E2M1 = mybir.dt.float4_e2m1fn_x4
ACT = mybir.ActivationFunctionType
ALU = mybir.AluOpType

P = 128
PACK = 4
QUADRANT = 32
SLOTS = J // 2
LIST_ROWS = 16
LINE = 16
BYTE_RUN = P // 2


def tile_list_outcomegatedcross_twotab_kernel(
    tc, xt_words, xt_scales, xo_words, xo_scales, w_words, w_scales, w2_words, w2_scales,
    wb_words, wb_scales, wc_words, wc_scales, so, sp, bo, so2, sp2, bo2,
    offs, offs2, offs3, offs4, offs5, offs6, out,
):
    nc = tc.nc
    with ExitStack() as ctx:
        sb = ctx.enter_context(tc.tile_pool(name="sb", bufs=1))
        ps = ctx.enter_context(tc.psum_pool(name="ps", bufs=1))

        def tile(name, shape, dtype):
            return sb.tile(shape, dtype, name=name, align_bytes=64)

        def load_list(name, src):
            offsets = tile(name, list(src.shape), U16)
            nc.sync.dma_start(offsets[:], src)
            return offsets

        def load_fp8_words(name, src, cols):
            words = tile(name, [P, cols], U32)
            nc.sync.dma_start(words[:].bitcast(I32), src[0].rearrange("p n t -> p (n t)").bitcast(I32))
            return words

        def load_fp4_words(name, src, cols):
            words = tile(name, [P, cols], U16)
            nc.sync.dma_start(words[:].bitcast(I32), src[0].bitcast(I32))
            return words

        def cleared(name, cols, engine):
            plane = tile(name, [P, cols], U8)
            engine.memset(plane[:].bitcast(I32), 0)
            return plane

        def load_plane(plane, src):
            for quad in range(4):
                nc.sync.dma_start(
                    plane[QUADRANT * quad : QUADRANT * quad + 4, :].bitcast(I32),
                    src[0, 4 * quad : 4 * quad + 4, :].bitcast(I32),
                )

        def load_folded(folded, src):
            halves = folded[:].bitcast(I32).rearrange("p (side c) -> p side c", side=2)
            rows = src[0].bitcast(I32).rearrange("(side low i) c -> low i side c", side=2, low=2)
            for low in range(2):
                nc.sync.dma_start(halves[QUADRANT * low : QUADRANT * low + 4, :, :], rows[low])

        def unfold(folded, cols):
            words = folded[:].bitcast(I32)
            nc.vector.tensor_copy(words[P // 2 : P, 0 : cols // 4], words[0 : P // 2, cols // 4 : cols // 2])

        def load_factor(name, src):
            factor = tile(name, [P, N // P], F32)
            with nc.allow_non_contiguous_dma(reason="one value a partition"):
                nc.sync.dma_start(factor[:], src.rearrange("(g p) o -> p (g o)", p=P))
            return factor

        w2_s = cleared("w2_s", 2 * R, nc.vector)
        xo_folded = tile("xo_f", [P, 2 * Z], U8)
        nc.gpsimd.memset(xo_folded[:, Z : 2 * Z].bitcast(I32), 0)
        nc.vector.memset(xo_folded[:, 0:Z].bitcast(I32), 0)
        w_s = cleared("w_s", 2 * R, nc.vector)
        xt_s = cleared("xt_s", T, nc.gpsimd)
        wb_s = cleared("wb_s", N, nc.vector)
        wc_s = cleared("wc_s", N, nc.vector)

        list2 = load_list("l2", offs2)
        list1 = load_list("l1", offs)
        load_folded(w2_s, w2_scales)
        xo_w = load_fp4_words("xo_w", xo_words, Z)
        load_folded(xo_folded, xo_scales)
        w2_w = load_fp8_words("w2_w", w2_words, R)
        w_w = load_fp4_words("w_w", w_words, R)
        load_folded(w_s, w_scales)
        xt_w = load_fp8_words("xt_w", xt_words, T)
        load_plane(xt_s, xt_scales)
        wb_w = load_fp8_words("wb_w", wb_words, N)
        wc_w = load_fp4_words("wc_w", wc_words, N)
        load_plane(wb_s, wb_scales)
        load_plane(wc_s, wc_scales)
        list6 = load_list("l6", offs6)
        slope2 = load_factor("sp2", sp2)
        offset2 = load_factor("bo2", bo2)
        list3 = load_list("l3", offs3)
        weight1 = load_factor("so", so)
        list4 = load_list("l4", offs4)
        slope1 = load_factor("sp", sp)
        offset1 = load_factor("bo", bo)
        list5 = load_list("l5", offs5)
        weight2 = load_factor("so2", so2)

        def gather(name, window, offsets, dtype):
            picked = tile(name, [P, J], dtype)
            nc.vector.tensor_copy(picked[:], window[:].indirect(offsets[:]))
            return picked

        def deal(name, src, dtype, copy, run):
            dealt = tile(name, [P, R], dtype)
            copy(
                dealt[:].rearrange("p (t c i) -> p c t i", t=PACK, i=run),
                src.rearrange("p (c i t) -> p c t i", t=PACK, i=run),
            )
            return dealt

        unfold(w2_s, R)
        w2_dealt_s = deal("w2_ds", w2_s[:, 0:R], U8, nc.vector.tensor_copy, BYTE_RUN)
        w2_dealt_w = deal("w2_d", w2_w[:], U32, nc.scalar.copy, LINE // 4)
        xo_picked_w = gather("xo_g", xo_w, list2, U16)
        xo_s = tile("xo_s", [P, Z], U8)
        for side in range(2):
            nc.vector.tensor_copy(
                xo_s[side * P // 2 : (side + 1) * P // 2, :].bitcast(I32),
                xo_folded[0 : P // 2, side * Z : (side + 1) * Z].bitcast(I32),
            )
        xo_picked_s = gather("xo_gs", xo_s, list2, U8)
        unfold(w_s, R)
        w_dealt_w = deal("w_d", w_w[:], U16, nc.scalar.copy, LINE // 2)
        w_dealt_s = deal("w_ds", w_s[:, 0:R], U8, nc.vector.tensor_copy, BYTE_RUN)
        xt_picked_w = gather("xt_g", xt_w, list1, U32)
        xt_picked_s = tile("xt_gs", [P, J], U8)
        for h in range(2):
            part = list1[:, h * SLOTS // LIST_ROWS : (h + 1) * SLOTS // LIST_ROWS]
            nc.vector.tensor_copy(xt_picked_s[:, h * SLOTS : (h + 1) * SLOTS], xt_s[:].indirect(part))

        def first_stage(name, dealt_w, dealt_s, dealt_fmt, picked_w, picked_s, picked_fmt, h):
            acc = ps.tile([P, PACK, SLOTS], F32, name=name)
            js = slice(h * SLOTS, (h + 1) * SLOTS)
            for t in range(PACK):
                ms = slice(t * P, (t + 1) * P)
                nc.tensor.matmul_mx(
                    out=acc[:, t, :], lhsT=dealt_w[:, ms].bitcast(dealt_fmt), lhsT_scale=dealt_s[:, ms],
                    rhs=picked_w[:, js].bitcast(picked_fmt), rhs_scale=picked_s[:, js], start=True, stop=True,
                )
            return acc

        b_sb = []
        for h in range(2):
            acc = first_stage("b_ps%d" % h, w2_dealt_w, w2_dealt_s, E5M2, xo_picked_w, xo_picked_s, E2M1, h)
            b_half = tile("b_sb%d" % h, [P, SLOTS, PACK], F32)
            nc.scalar.copy(b_half[:], acc[:].rearrange("p t j -> p j t"))
            b_sb.append(b_half)
        hid = []
        for h in range(2):
            acc = first_stage("a_ps%d" % h, w_dealt_w, w_dealt_s, E2M1, xt_picked_w, xt_picked_s, E4M3, h)
            hid_half = tile("hid%d" % h, [P, SLOTS, PACK], BF16)
            nc.vector.tensor_tensor(hid_half[:], acc[:].rearrange("p t j -> p j t"), b_sb[h][:], ALU.max)
            hid.append(hid_half)
        hid_mx = []
        for h in range(2):
            codes = tile("hq%d" % h, [P, SLOTS], U32)
            scales = tile("hs%d" % h, [P, SLOTS], U8)
            nc.vector.quantize_mx(
                out=codes[:].bitcast(E4M3), scales=scales[:], in_=hid[h][:].rearrange("p j t -> p (j t)")
            )
            hid_mx.append((codes, scales))

        outcome_ps = {}
        for g in range(N // P):
            for name in ("p", "q"):
                outcome_ps[name, g] = ps.tile([P, J], F32, name="%s_ps%d" % (name, g))
        for g in range(N // P):
            ns = slice(g * P, (g + 1) * P)
            for name, words, plane, fmt in (("p", wb_w, wb_s, E5M2), ("q", wc_w, wc_s, E2M1)):
                for h in range(2):
                    codes, scales = hid_mx[h]
                    nc.tensor.matmul_mx(
                        out=outcome_ps[name, g][:, h * SLOTS : (h + 1) * SLOTS],
                        lhsT=words[:, ns].bitcast(fmt), lhsT_scale=plane[:, ns],
                        rhs=codes[:].bitcast(E4M3), rhs_scale=scales[:], start=True, stop=True,
                    )

        outcome = {}
        for g in range(N // P):
            for name in ("p", "q"):
                window = tile("%s_sb%d" % (name, g), [P, J], F32)
                nc.vector.tensor_copy(window[:], outcome_ps[name, g][:])
                outcome[name, g] = window

        for g in range(N // P):
            col = slice(g, g + 1)
            gate2 = tile("gate2_%d" % g, [P, O], F32)
            nc.scalar.activation(out=gate2[:], in_=outcome["p", g][:].indirect(list6[:]), func=ACT.Sigmoid,
                                 bias=offset2[:, col], scale=slope2[:, col])
            value1 = tile("val1_%d" % g, [P, O], F32)
            nc.scalar.activation(out=value1[:], in_=outcome["p", g][:].indirect(list3[:]), func=ACT.Copy,
                                 scale=weight1[:, col])
            gate1 = tile("gate1_%d" % g, [P, O], F32)
            nc.scalar.activation(out=gate1[:], in_=outcome["q", g][:].indirect(list4[:]), func=ACT.Sigmoid,
                                 bias=offset1[:, col], scale=slope1[:, col])
            value2 = tile("val2_%d" % g, [P, O], F32)
            nc.scalar.activation(out=value2[:], in_=outcome["q", g][:].indirect(list5[:]), func=ACT.Copy,
                                 scale=weight2[:, col])
            gated1 = tile("t1_%d" % g, [P, O], F32)
            nc.vector.tensor_tensor(gated1[:], value1[:], gate1[:], ALU.mult)
            gated2 = tile("t2_%d" % g, [P, O], F32)
            nc.vector.tensor_tensor(gated2[:], value2[:], gate2[:], ALU.mult)
            y = tile("y_%d" % g, [P, O], F32)
            nc.vector.tensor_tensor(y[:], gated1[:], gated2[:], ALU.subtract)
            nc.sync.dma_start(out[g * P : (g + 1) * P, :], y[:])
